import numpy as np
import ml_dtypes


def mxq(x, axis, fmt="e4m3"):
    dtype, down = {"e4m3": (ml_dtypes.float8_e4m3fn, 7), "e5m2": (ml_dtypes.float8_e5m2, 14)}[fmt]
    v = np.moveaxis(np.asarray(x, np.float32).astype(ml_dtypes.bfloat16).astype(np.float64), axis, -1)
    blocks = v.reshape(v.shape[:-1] + (-1, 32))
    amax = np.abs(blocks).max(-1, keepdims=True)
    byte = np.maximum(np.where(amax > 0, np.frexp(amax)[1] - 1 + 127, 0) - down, 1)
    scale = np.exp2(byte - 127.0)
    codes = (blocks / scale).astype(np.float32).astype(dtype).astype(np.float64)
    return np.moveaxis((codes * scale).reshape(v.shape), -1, axis)


WIDE = False


def mx_kscale(k):
    if not WIDE:
        return np.ones(k)
    levels = np.array([10, -10, 5, -5, 0])
    if k % 512:
        return np.exp2(np.random.permutation(np.resize(levels, k // 32))).repeat(32)
    a = np.empty((k // 512, 16))
    for p in range(k // 512):
        a[p, :8] = np.random.permutation(np.resize(levels, 8))
        for g in range(8):
            far = levels[np.abs(levels - a[p, g]) >= 10]
            a[p, g + 8] = far[np.random.randint(len(far))]
    return np.exp2(a.ravel()).repeat(32)


def f64(x):
    return np.asarray(x).astype(np.float64)


def striped(idx):
    return np.tile(idx.reshape(-1, 16).T, (8, 1)).astype(np.uint16)


def unstriped(offs):
    return offs[:16].T.reshape(-1).astype(np.int64)


def silu(v):
    return v / (1.0 + np.exp(-np.maximum(v, -700.0)))


K, T, E, C, H, N = 1536, 1024, 4, 128, 512, 256


def by_expert(wq, xq):
    return np.concatenate([wq[e].T @ xq[:, e * C:(e + 1) * C] for e in range(E)], axis=1)


def setup_inputs():
    n = np.random.standard_normal
    s = mx_kscale(K)[:, None]
    u = mx_kscale(H)
    return {
        "xT": (n((K, T)) * s).astype(np.float32),
        "w1": (n((E, K, H)) / np.sqrt(K) / s[None]).astype(np.float32),
        "w3": (n((E, K, H)) / np.sqrt(K) / s[None] * u[None, None, :]).astype(np.float32),
        "w2": (n((E, H, N)) / np.sqrt(H) / u[None, :, None]).astype(np.float32),
        "gate": np.tile(np.random.uniform(0.2, 1.0, E * C), (N, 1)).astype(np.float32),
        "offs": striped(np.random.permutation(T)[:E * C]),
    }


def reference(xT, w1, w3, w2, gate, offs):
    idx = unstriped(offs)
    xq = mxq(f64(xT)[:, idx], 0, "e4m3")
    h = silu(by_expert(mxq(f64(w1), 1, "e4m3"), xq))
    h = h * by_expert(mxq(f64(w3), 1, "e4m3"), xq)
    y = by_expert(mxq(f64(w2), 1, "e4m3"), mxq(h, 0, "e4m3"))
    out = np.zeros((N, T))
    out[:, idx] = f64(gate) * y
    return out

@@ -1,0 +1,148 @@
+from contextlib import ExitStack
+
+import concourse.mybir as mybir
+
+K, T, E, C, H, N = 1536, 1024, 4, 128, 512, 256
+S = E * C
+P = 128
+J = 4
+G = K // (P * J)
+
+F32 = mybir.dt.float32
+BF16 = mybir.dt.bfloat16
+U32 = mybir.dt.uint32
+U16 = mybir.dt.uint16
+U8 = mybir.dt.uint8
+FP8X4 = mybir.dt.float8_e4m3fn_x4
+MULT = mybir.AluOpType.mult
+SILU = mybir.ActivationFunctionType.Silu
+
+FLOPS = 2 * S * (2 * K * H + H * N)
+
+
+def tile_routed_moe_kernel(tc, xT, w1, w3, w2, gate, offs, out):
+    nc = tc.nc
+    with ExitStack() as ctx:
+        keep = ctx.enter_context(tc.tile_pool(name="keep", bufs=1))
+        rawp = ctx.enter_context(tc.tile_pool(name="rawp", bufs=8))
+        grpp = ctx.enter_context(tc.tile_pool(name="grpp", bufs=6))
+        wq = ctx.enter_context(tc.tile_pool(name="wq", bufs=3))
+        work = ctx.enter_context(tc.tile_pool(name="work", bufs=2))
+        psum = ctx.enter_context(tc.psum_pool(name="psum", bufs=2))
+
+        lst = keep.tile([P, S // 16], U16, name="lst")
+
+        warm = keep.tile([P, 1], F32, name="warm")
+        nc.vector.memset(warm[:], 0.0)
+        nc.scalar.activation(warm[:], warm[:], SILU)
+        wins = []
+        for b in range(2):
+            win = keep.tile([P, T], F32, name=f"win{b}")
+            nc.vector.memset(win[:], 0.0)
+            wins.append(win)
+
+        def copy(engine, dst, src):
+            if engine == 0:
+                nc.vector.tensor_copy(dst, src)
+            else:
+                nc.scalar.copy(dst, src)
+
+        xv = xT.rearrange("(g p j) n -> g p j n", p=P, j=J)
+        gw = keep.tile([P, G, S], U32, name="gw", align_bytes=64)
+        gs = keep.tile([P, G, S], U8, name="gs", align_bytes=64)
+        for g in range(G):
+            xw = keep.tile([P, T], U32, name=f"xw{g}", align_bytes=64)
+            xs = keep.tile([P, T], U8, name=f"xs{g}", align_bytes=64)
+            for half in range(2):
+                cols = slice(512 * half, 512 * half + 512)
+                raw = rawp.tile([P, J, 512], F32, name="raw")
+                nc.sync.dma_start(raw[:], xv[g, :, :, cols])
+                if g == 0 and half == 0:
+                    nc.sync.dma_start(lst[:], offs)
+                grp = grpp.tile([P, 512, J], BF16, name="grp", align_bytes=64)
+                copy(half, grp[:], raw[:].rearrange("p j w -> p w j"))
+                nc.vector.quantize_mx(out=xw[:, cols].bitcast(FP8X4), scales=xs[:, cols], in_=grp[:].rearrange("p w j -> p (w j)"))
+            nc.vector.tensor_copy(gw[:, g, :], xw[:].indirect(lst[:]))
+            nc.vector.tensor_copy(gs[:, g, :], xs[:].indirect(lst[:]))
+
+        gt = keep.tile([P, 2, S], F32, name="gt")
+        w1v = w1.rearrange("e (g p j) h -> e g p j h", p=P, j=J)
+        w3v = w3.rearrange("e (g p j) h -> e g p j h", p=P, j=J)
+        w2v = w2.rearrange("e (p j) n -> e p j n", j=J)
+
+        for e in range(E):
+            slots = slice(C * e, C * e + C)
+            hid = []
+            for which, wv in enumerate((w1v, w3v)):
+                wc = wq.tile([P, G, H], U32, name=f"wc{which}", align_bytes=64)
+                ws = wq.tile([P, G, H], U8, name=f"ws{which}", align_bytes=64)
+                for g in range(G):
+                    grp = grpp.tile([P, H, J], BF16, name="grp", align_bytes=64)
+                    dst = grp[:].rearrange("p (t m) j -> p m t j", t=4)
+                    if e == E - 1 and which == 1 and g == G - 1:
+                        for part in range(2):
+                            piece = rawp.tile([P, J, H // 2], F32, name="piece")
+                            nc.sync.dma_start(piece[:], wv[e, g, :, :, 256 * part:256 * part + 256])
+                            src = piece[:].rearrange("p j (m t) -> p m t j", t=4)
+                            for eng in range(2):
+                                tt = slice(2 * eng, 2 * eng + 2)
+                                copy(eng, dst[:, 64 * part:64 * part + 64, tt, :], src[:, :, tt, :])
+                        for u in range(2):
+                            cc = slice(256 * u, 256 * u + 256)
+                            nc.vector.quantize_mx(out=wc[:, g, cc].bitcast(FP8X4), scales=ws[:, g, cc], in_=grp[:, cc, :].rearrange("p w j -> p (w j)"))
+                        continue
+                    raw = rawp.tile([P, J, H], F32, name="raw")
+                    nc.sync.dma_start(raw[:], wv[e, g])
+                    src = raw[:].rearrange("p j (m t) -> p m t j", t=4)
+                    copy((G * which + g) % 2, dst, src)
+                    nc.vector.quantize_mx(out=wc[:, g, :].bitcast(FP8X4), scales=ws[:, g, :], in_=grp[:].rearrange("p w j -> p (w j)"))
+                acc = psum.tile([P, 4, C], F32, name=f"acc{which}")
+                for t in range(4):
+                    for g in range(G):
+                        nc.tensor.matmul_mx(
+                            out=acc[:, t, :],
+                            lhsT=wc[:, g, P * t:P * t + P].bitcast(FP8X4),
+                            lhsT_scale=ws[:, g, P * t:P * t + P],
+                            rhs=gw[:, g, slots].bitcast(FP8X4),
+                            rhs_scale=gs[:, g, slots],
+                            start=(g == 0),
+                            stop=(g == G - 1),
+                        )
+                if which == 0:
+                    sil = work.tile([P, 4, C], F32, name="sil")
+                    nc.scalar.activation(sil[:], acc[:], SILU)
+                else:
+                    hb = work.tile([P, C, 4], BF16, name="hb", align_bytes=64)
+                    nc.vector.tensor_tensor(hb[:], sil[:].rearrange("p t c -> p c t"), acc[:].rearrange("p t c -> p c t"), MULT)
+                    hc = work.tile([P, C], U32, name="hc", align_bytes=64)
+                    hs = work.tile([P, C], U8, name="hs", align_bytes=64)
+                    nc.vector.quantize_mx(out=hc[:].bitcast(FP8X4), scales=hs[:], in_=hb[:].rearrange("p c t -> p (c t)"))
+            raw2 = work.tile([P, J, N], F32, name="raw2")
+            nc.sync.dma_start(raw2[:], w2v[e])
+            if e == 0:
+                nc.sync.dma_start(gt[:], gate.rearrange("(b p) s -> p b s", p=P))
+            grp2 = work.tile([P, N, J], BF16, name="grp2", align_bytes=64)
+            nc.scalar.copy(grp2[:], raw2[:].rearrange("p j n -> p n j"))
+            vc = work.tile([P, N], U32, name="vc", align_bytes=64)
+            vs = work.tile([P, N], U8, name="vs", align_bytes=64)
+            nc.vector.quantize_mx(out=vc[:].bitcast(FP8X4), scales=vs[:], in_=grp2[:].rearrange("p n j -> p (n j)"))
+            y = psum.tile([P, 2, C], F32, name="y")
+            for b in range(2):
+                nc.tensor.matmul_mx(
+                    out=y[:, b, :],
+                    lhsT=vc[:, P * b:P * b + P].bitcast(FP8X4),
+                    lhsT_scale=vs[:, P * b:P * b + P],
+                    rhs=hc[:].bitcast(FP8X4),
+                    rhs_scale=hs[:],
+                    start=True,
+                    stop=True,
+                )
+            yg = work.tile([P, 2, C], F32, name="yg")
+            if e < E - 1:
+                nc.vector.tensor_tensor(yg[:], y[:], gt[:, :, slots], MULT)
+            for b in range(2):
+                if e == E - 1:
+                    nc.vector.tensor_tensor(yg[:, b, :], y[:, b, :], gt[:, b, slots], MULT)
+                nc.vector.tensor_copy(wins[b][:].indirect(lst[:, 8 * e:8 * e + 8]), yg[:, b, :])
+        for b in range(2):
+            nc.sync.dma_start(out[P * b:P * b + P, :], wins[b][:])

@@ -24,9 +24,10 @@ def tile_routed_moe_kernel(tc, xT, w1, w3, w2, gate, offs, out):
     nc = tc.nc
     with ExitStack() as ctx:
         keep = ctx.enter_context(tc.tile_pool(name="keep", bufs=1))
-        rawp = ctx.enter_context(tc.tile_pool(name="rawp", bufs=8))
+        rawp = ctx.enter_context(tc.tile_pool(name="rawp", bufs=7))
+        xrawp = ctx.enter_context(tc.tile_pool(name="xrawp", bufs=3))
         grpp = ctx.enter_context(tc.tile_pool(name="grpp", bufs=6))
-        wq = ctx.enter_context(tc.tile_pool(name="wq", bufs=3))
+        wq = ctx.enter_context(tc.tile_pool(name="wq", bufs=2))
         work = ctx.enter_context(tc.tile_pool(name="work", bufs=2))
         psum = ctx.enter_context(tc.psum_pool(name="psum", bufs=2))
 
@@ -53,14 +54,14 @@ def tile_routed_moe_kernel(tc, xT, w1, w3, w2, gate, offs, out):
         for g in range(G):
             xw = keep.tile([P, T], U32, name=f"xw{g}", align_bytes=64)
             xs = keep.tile([P, T], U8, name=f"xs{g}", align_bytes=64)
+            xraw = xrawp.tile([P, J, T], F32, name="xraw")
+            nc.sync.dma_start(xraw[:], xv[g])
+            if g == 0:
+                nc.sync.dma_start(lst[:], offs)
             for half in range(2):
                 cols = slice(512 * half, 512 * half + 512)
-                raw = rawp.tile([P, J, 512], F32, name="raw")
-                nc.sync.dma_start(raw[:], xv[g, :, :, cols])
-                if g == 0 and half == 0:
-                    nc.sync.dma_start(lst[:], offs)
                 grp = grpp.tile([P, 512, J], BF16, name="grp", align_bytes=64)
-                copy(half, grp[:], raw[:].rearrange("p j w -> p w j"))
+                copy(1 if g == 1 else half, grp[:], xraw[:, :, cols].rearrange("p j w -> p w j"))
                 nc.vector.quantize_mx(out=xw[:, cols].bitcast(FP8X4), scales=xs[:, cols], in_=grp[:].rearrange("p w j -> p (w j)"))
             nc.vector.tensor_copy(gw[:, g, :], xw[:].indirect(lst[:]))
             nc.vector.tensor_copy(gs[:, g, :], xs[:].indirect(lst[:]))
@@ -81,7 +82,7 @@ def tile_routed_moe_kernel(tc, xT, w1, w3, w2, gate, offs, out):
                     dst = grp[:].rearrange("p (t m) j -> p m t j", t=4)
                     if e == E - 1 and which == 1 and g == G - 1:
                         for part in range(2):
-                            piece = rawp.tile([P, J, H // 2], F32, name="piece")
+                            piece = work.tile([P, J, H // 2], F32, name="piece")
                             nc.sync.dma_start(piece[:], wv[e, g, :, :, 256 * part:256 * part + 256])
                             src = piece[:].rearrange("p j (m t) -> p m t j", t=4)
                             for eng in range(2):
@@ -94,7 +95,7 @@ def tile_routed_moe_kernel(tc, xT, w1, w3, w2, gate, offs, out):
                     raw = rawp.tile([P, J, H], F32, name="raw")
                     nc.sync.dma_start(raw[:], wv[e, g])
                     src = raw[:].rearrange("p j (m t) -> p m t j", t=4)
-                    copy((G * which + g) % 2, dst, src)
+                    copy(0 if g == 1 else 1, dst, src)
                     nc.vector.quantize_mx(out=wc[:, g, :].bitcast(FP8X4), scales=ws[:, g, :], in_=grp[:].rearrange("p w j -> p (w j)"))
                 acc = psum.tile([P, 4, C], F32, name=f"acc{which}")
                 for t in range(4):

@@ -7,6 +7,7 @@ S = E * C
 P = 128
 J = 4
 G = K // (P * J)
+NB = N // P
 
 F32 = mybir.dt.float32
 BF16 = mybir.dt.bfloat16
@@ -17,118 +18,103 @@ FP8X4 = mybir.dt.float8_e4m3fn_x4
 MULT = mybir.AluOpType.mult
 SILU = mybir.ActivationFunctionType.Silu
 
+V_M_LAST = 96
+
 FLOPS = 2 * S * (2 * K * H + H * N)
+
+
+def flat(grouped):
+    return grouped.rearrange("p w j -> p (w j)")
 
 
 def tile_routed_moe_kernel(tc, xT, w1, w3, w2, gate, offs, out):
     nc = tc.nc
+    x_rows = xT.rearrange("(g p j) n -> g p (j n)", p=P, j=J)
+    w_rows = [w.rearrange("e (g p j) h -> e g p (j h)", p=P, j=J) for w in (w1, w3)]
+    w2_rows = w2.rearrange("e (p j) n -> e p (j n)", j=J)
+
     with ExitStack() as ctx:
         keep = ctx.enter_context(tc.tile_pool(name="keep", bufs=1))
-        rawp = ctx.enter_context(tc.tile_pool(name="rawp", bufs=7))
         xrawp = ctx.enter_context(tc.tile_pool(name="xrawp", bufs=3))
-        grpp = ctx.enter_context(tc.tile_pool(name="grpp", bufs=6))
+        rawp = ctx.enter_context(tc.tile_pool(name="rawp", bufs=7))
+        grpp = ctx.enter_context(tc.tile_pool(name="grpp", bufs=3))
+        grpv = ctx.enter_context(tc.tile_pool(name="grpv", bufs=2))
         wq = ctx.enter_context(tc.tile_pool(name="wq", bufs=2))
         work = ctx.enter_context(tc.tile_pool(name="work", bufs=2))
         psum = ctx.enter_context(tc.psum_pool(name="psum", bufs=2))
 
         lst = keep.tile([P, S // 16], U16, name="lst")
-
-        warm = keep.tile([P, 1], F32, name="warm")
-        nc.vector.memset(warm[:], 0.0)
-        nc.scalar.activation(warm[:], warm[:], SILU)
+        gt = keep.tile([P, NB, S], F32, name="gt")
         wins = []
-        for b in range(2):
+        for b in range(NB):
             win = keep.tile([P, T], F32, name=f"win{b}")
             nc.vector.memset(win[:], 0.0)
             wins.append(win)
+        warm = keep.tile([P, 1], F32, name="warm")
+        nc.vector.memset(warm[:], 0.0)
+        nc.scalar.activation(warm[:], warm[:], SILU)
 
-        def copy(engine, dst, src):
-            if engine == 0:
-                nc.vector.tensor_copy(dst, src)
-            else:
-                nc.scalar.copy(dst, src)
-
-        xv = xT.rearrange("(g p j) n -> g p j n", p=P, j=J)
         gw = keep.tile([P, G, S], U32, name="gw", align_bytes=64)
         gs = keep.tile([P, G, S], U8, name="gs", align_bytes=64)
         for g in range(G):
-            xw = keep.tile([P, T], U32, name=f"xw{g}", align_bytes=64)
-            xs = keep.tile([P, T], U8, name=f"xs{g}", align_bytes=64)
-            xraw = xrawp.tile([P, J, T], F32, name="xraw")
-            nc.sync.dma_start(xraw[:], xv[g])
+            xraw = xrawp.tile([P, J * T], F32, name="xraw")
+            nc.sync.dma_start(xraw[:], x_rows[g])
             if g == 0:
                 nc.sync.dma_start(lst[:], offs)
+            xin = xraw[:].rearrange("p (j n) -> p n j", j=J)
+            xw = keep.tile([P, T], U32, name=f"xw{g}", align_bytes=64)
+            xs = keep.tile([P, T], U8, name=f"xs{g}", align_bytes=64)
             for half in range(2):
-                cols = slice(512 * half, 512 * half + 512)
-                grp = grpp.tile([P, 512, J], BF16, name="grp", align_bytes=64)
-                copy(1 if g == 1 else half, grp[:], xraw[:, :, cols].rearrange("p j w -> p w j"))
-                nc.vector.quantize_mx(out=xw[:, cols].bitcast(FP8X4), scales=xs[:, cols], in_=grp[:].rearrange("p w j -> p (w j)"))
+                t0 = half * H
+                cols = slice(t0, t0 + H)
+                if (g, half) in ((0, 0), (2, 0)):
+                    grp = grpv.tile([P, H, J], BF16, name="grp_v", align_bytes=64)
+                    nc.vector.tensor_copy(grp[:], xin[:, cols, :])
+                else:
+                    grp = grpp.tile([P, H, J], BF16, name="grp_s", align_bytes=64)
+                    nc.scalar.copy(grp[:], xin[:, cols, :])
+                nc.vector.quantize_mx(out=xw[:, cols].bitcast(FP8X4), scales=xs[:, cols], in_=flat(grp[:]))
             nc.vector.tensor_copy(gw[:, g, :], xw[:].indirect(lst[:]))
             nc.vector.tensor_copy(gs[:, g, :], xs[:].indirect(lst[:]))
 
-        gt = keep.tile([P, 2, S], F32, name="gt")
-        w1v = w1.rearrange("e (g p j) h -> e g p j h", p=P, j=J)
-        w3v = w3.rearrange("e (g p j) h -> e g p j h", p=P, j=J)
-        w2v = w2.rearrange("e (p j) n -> e p j n", j=J)
+        state = {}
 
-        for e in range(E):
-            slots = slice(C * e, C * e + C)
-            hid = []
-            for which, wv in enumerate((w1v, w3v)):
-                wc = wq.tile([P, G, H], U32, name=f"wc{which}", align_bytes=64)
-                ws = wq.tile([P, G, H], U8, name=f"ws{which}", align_bytes=64)
+        def slots(e):
+            return slice(C * e, C * e + C)
+
+        def first_layer(e, which):
+            wc, ws = state["w", e, which]
+            acc = psum.tile([P, 4, C], F32, name=f"acc{which}")
+            for t in range(4):
                 for g in range(G):
-                    grp = grpp.tile([P, H, J], BF16, name="grp", align_bytes=64)
-                    dst = grp[:].rearrange("p (t m) j -> p m t j", t=4)
-                    if e == E - 1 and which == 1 and g == G - 1:
-                        for part in range(2):
-                            piece = work.tile([P, J, H // 2], F32, name="piece")
-                            nc.sync.dma_start(piece[:], wv[e, g, :, :, 256 * part:256 * part + 256])
-                            src = piece[:].rearrange("p j (m t) -> p m t j", t=4)
-                            for eng in range(2):
-                                tt = slice(2 * eng, 2 * eng + 2)
-                                copy(eng, dst[:, 64 * part:64 * part + 64, tt, :], src[:, :, tt, :])
-                        for u in range(2):
-                            cc = slice(256 * u, 256 * u + 256)
-                            nc.vector.quantize_mx(out=wc[:, g, cc].bitcast(FP8X4), scales=ws[:, g, cc], in_=grp[:, cc, :].rearrange("p w j -> p (w j)"))
-                        continue
-                    raw = rawp.tile([P, J, H], F32, name="raw")
-                    nc.sync.dma_start(raw[:], wv[e, g])
-                    src = raw[:].rearrange("p j (m t) -> p m t j", t=4)
-                    copy(0 if g == 1 else 1, dst, src)
-                    nc.vector.quantize_mx(out=wc[:, g, :].bitcast(FP8X4), scales=ws[:, g, :], in_=grp[:].rearrange("p w j -> p (w j)"))
-                acc = psum.tile([P, 4, C], F32, name=f"acc{which}")
-                for t in range(4):
-                    for g in range(G):
-                        nc.tensor.matmul_mx(
-                            out=acc[:, t, :],
-                            lhsT=wc[:, g, P * t:P * t + P].bitcast(FP8X4),
-                            lhsT_scale=ws[:, g, P * t:P * t + P],
-                            rhs=gw[:, g, slots].bitcast(FP8X4),
-                            rhs_scale=gs[:, g, slots],
-                            start=(g == 0),
-                            stop=(g == G - 1),
-                        )
-                if which == 0:
-                    sil = work.tile([P, 4, C], F32, name="sil")
-                    nc.scalar.activation(sil[:], acc[:], SILU)
-                else:
-                    hb = work.tile([P, C, 4], BF16, name="hb", align_bytes=64)
-                    nc.vector.tensor_tensor(hb[:], sil[:].rearrange("p t c -> p c t"), acc[:].rearrange("p t c -> p c t"), MULT)
-                    hc = work.tile([P, C], U32, name="hc", align_bytes=64)
-                    hs = work.tile([P, C], U8, name="hs", align_bytes=64)
-                    nc.vector.quantize_mx(out=hc[:].bitcast(FP8X4), scales=hs[:], in_=hb[:].rearrange("p c t -> p (c t)"))
-            raw2 = work.tile([P, J, N], F32, name="raw2")
-            nc.sync.dma_start(raw2[:], w2v[e])
-            if e == 0:
-                nc.sync.dma_start(gt[:], gate.rearrange("(b p) s -> p b s", p=P))
-            grp2 = work.tile([P, N, J], BF16, name="grp2", align_bytes=64)
-            nc.scalar.copy(grp2[:], raw2[:].rearrange("p j n -> p n j"))
-            vc = work.tile([P, N], U32, name="vc", align_bytes=64)
-            vs = work.tile([P, N], U8, name="vs", align_bytes=64)
-            nc.vector.quantize_mx(out=vc[:].bitcast(FP8X4), scales=vs[:], in_=grp2[:].rearrange("p n j -> p (n j)"))
-            y = psum.tile([P, 2, C], F32, name="y")
-            for b in range(2):
+                    nc.tensor.matmul_mx(
+                        out=acc[:, t, :],
+                        lhsT=wc[:, g, P * t:P * t + P].bitcast(FP8X4),
+                        lhsT_scale=ws[:, g, P * t:P * t + P],
+                        rhs=gw[:, g, slots(e)].bitcast(FP8X4),
+                        rhs_scale=gs[:, g, slots(e)],
+                        start=(g == 0),
+                        stop=(g == G - 1),
+                    )
+            state["acc", e, which] = acc
+
+        def silu(e):
+            sil = work.tile([P, 4, C], F32, name="sil")
+            nc.scalar.activation(sil[:], state["acc", e, 0][:], SILU)
+            state["sil", e] = sil
+
+        def product(e):
+            hb = work.tile([P, C, 4], BF16, name="hb", align_bytes=64)
+            nc.vector.tensor_tensor(hb[:], state["sil", e][:].rearrange("p t c -> p c t"), state["acc", e, 1][:].rearrange("p t c -> p c t"), MULT)
+            state["hb", e] = hb
+
+        def quantise_hidden(e):
+            hc = work.tile([P, C], U32, name="hc", align_bytes=64)
+            hs = work.tile([P, C], U8, name="hs", align_bytes=64)
+            nc.vector.quantize_mx(out=hc[:].bitcast(FP8X4), scales=hs[:], in_=flat(state["hb", e][:]))
+            vc, vs = state["w2", e]
+            y = psum.tile([P, NB, C], F32, name="y")
+            for b in range(NB):
                 nc.tensor.matmul_mx(
                     out=y[:, b, :],
                     lhsT=vc[:, P * b:P * b + P].bitcast(FP8X4),
@@ -138,12 +124,80 @@ def tile_routed_moe_kernel(tc, xT, w1, w3, w2, gate, offs, out):
                     start=True,
                     stop=True,
                 )
-            yg = work.tile([P, 2, C], F32, name="yg")
-            if e < E - 1:
-                nc.vector.tensor_tensor(yg[:], y[:], gt[:, :, slots], MULT)
-            for b in range(2):
-                if e == E - 1:
-                    nc.vector.tensor_tensor(yg[:, b, :], y[:, b, :], gt[:, b, slots], MULT)
-                nc.vector.tensor_copy(wins[b][:].indirect(lst[:, 8 * e:8 * e + 8]), yg[:, b, :])
-        for b in range(2):
+            state["y", e] = y
+
+        def gated(e):
+            yg = work.tile([P, NB, C], F32, name="yg")
+            nc.vector.tensor_tensor(yg[:], state["y", e][:], gt[:, :, slots(e)], MULT)
+            state["yg", e] = yg
+
+        def scatter(e, b):
+            nc.vector.tensor_copy(wins[b][:].indirect(lst[:, 8 * e:8 * e + 8]), state["yg", e][:, b, :])
+
+        items = []
+        for e in range(E):
+            items.extend([(e, which, g) for which in range(2) for g in range(G)])
+            items.append((e, 2, 0))
+        later = []
+        pending = []
+        for step, (e, which, g) in enumerate(items):
+            last = e == E - 1
+            if which == 2:
+                raw = work.tile([P, J * N], F32, name="raw2")
+                nc.sync.dma_start(raw[:], w2_rows[e])
+                if e == 0:
+                    nc.sync.dma_start(gt[:], gate.rearrange("(b p) s -> p b s", p=P))
+                grp = work.tile([P, N, J], BF16, name="grp2", align_bytes=64)
+                nc.scalar.copy(grp[:], raw[:].rearrange("p (j n) -> p n j", j=J))
+                vc = work.tile([P, N], U32, name="vc", align_bytes=64)
+                vs = work.tile([P, N], U8, name="vs", align_bytes=64)
+                state["w2", e] = (vc, vs)
+                jobs = [(vc[:], vs[:], grp[:])]
+            else:
+                raw = rawp.tile([P, J * H], F32, name="raw")
+                nc.sync.dma_start(raw[:], w_rows[which][e, g])
+                if g == 0:
+                    wc = wq.tile([P, G, H], U32, name=f"wc{which}", align_bytes=64)
+                    ws = wq.tile([P, G, H], U8, name=f"ws{which}", align_bytes=64)
+                    state["w", e, which] = (wc, ws)
+                wc, ws = state["w", e, which]
+                on_v = (G * which + g) in (1, 4, 5)
+                grp = grpv.tile([P, H, J], BF16, name="grp_v", align_bytes=64) if on_v else grpp.tile([P, H, J], BF16, name="grp_s", align_bytes=64)
+                src = raw[:].rearrange("p (j m t) -> p m t j", j=J, t=4)
+                dst = grp[:].rearrange("p (t m) j -> p m t j", t=4)
+                final = last and which == 1 and g == G - 1
+                m = (V_M_LAST if final else P) if on_v else 0
+                if m:
+                    nc.vector.tensor_copy(dst[:, :m], src[:, :m])
+                if m < P:
+                    nc.scalar.copy(dst[:, m:], src[:, m:])
+                parts = 2 if final else 1
+                width = H // parts
+                jobs = [(wc[:, g, u * width:u * width + width], ws[:, g, u * width:u * width + width], grp[:, u * width:u * width + width, :]) for u in range(parts)]
+            for codes, scales, grouped in pending:
+                nc.vector.quantize_mx(out=codes.bitcast(FP8X4), scales=scales, in_=flat(grouped))
+            pending = jobs
+            for due, function, args in later:
+                if due == step:
+                    function(*args)
+            if which < 2 and g == G - 1:
+                later.append((step + 1, first_layer, (e, which)))
+                if which == 0:
+                    later.append((step + 3, silu, (e,)))
+                elif not last:
+                    later.append((step + 2, product, (e,)))
+                    later.append((step + 3, quantise_hidden, (e,)))
+                    later.append((step + 4, gated, (e,)))
+                    later.append((step + 5, scatter, (e, 0)))
+                    later.append((step + 6, scatter, (e, 1)))
+        for codes, scales, grouped in pending:
+            nc.vector.quantize_mx(out=codes.bitcast(FP8X4), scales=scales, in_=flat(grouped))
+        e = E - 1
+        product(e)
+        quantise_hidden(e)
+        yg = work.tile([P, NB, C], F32, name="yg")
+        for b in range(NB):
+            nc.vector.tensor_tensor(yg[:, b, :], state["y", e][:, b, :], gt[:, b, slots(e)], MULT)
+            state["yg", e] = yg
+            scatter(e, b)
             nc.sync.dma_start(out[P * b:P * b + P, :], wins[b][:])

@@ -18,7 +18,7 @@ FP8X4 = mybir.dt.float8_e4m3fn_x4
 MULT = mybir.AluOpType.mult
 SILU = mybir.ActivationFunctionType.Silu
 
-V_M_LAST = 96
+V_M_LAST = 72
 
 FLOPS = 2 * S * (2 * K * H + H * N)
 
@@ -142,40 +142,53 @@ def tile_routed_moe_kernel(tc, xT, w1, w3, w2, gate, offs, out):
         pending = []
         for step, (e, which, g) in enumerate(items):
             last = e == E - 1
+            if last and which == 2:
+                for codes, scales, grouped in pending:
+                    nc.vector.quantize_mx(out=codes.bitcast(FP8X4), scales=scales, in_=flat(grouped))
             if which == 2:
                 raw = work.tile([P, J * N], F32, name="raw2")
                 nc.sync.dma_start(raw[:], w2_rows[e])
                 if e == 0:
                     nc.sync.dma_start(gt[:], gate.rearrange("(b p) s -> p b s", p=P))
                 grp = work.tile([P, N, J], BF16, name="grp2", align_bytes=64)
-                nc.scalar.copy(grp[:], raw[:].rearrange("p (j n) -> p n j", j=J))
+                n0 = N // 2 if last else 0
+                src = raw[:].rearrange("p (j n) -> p n j", j=J)
+                if last:
+                    nc.vector.tensor_copy(grp[:, :n0], src[:, :n0])
+                nc.scalar.copy(grp[:, n0:], src[:, n0:])
                 vc = work.tile([P, N], U32, name="vc", align_bytes=64)
                 vs = work.tile([P, N], U8, name="vs", align_bytes=64)
                 state["w2", e] = (vc, vs)
                 jobs = [(vc[:], vs[:], grp[:])]
             else:
+                final = last and which == 1 and g == G - 1
                 raw = rawp.tile([P, J * H], F32, name="raw")
-                nc.sync.dma_start(raw[:], w_rows[which][e, g])
+                pieces = 2 if final else 1
+                for q in range(pieces):
+                    part = slice(q * J * H // pieces, (q + 1) * J * H // pieces)
+                    nc.sync.dma_start(raw[:, part], w_rows[which][e, g, :, part])
                 if g == 0:
                     wc = wq.tile([P, G, H], U32, name=f"wc{which}", align_bytes=64)
                     ws = wq.tile([P, G, H], U8, name=f"ws{which}", align_bytes=64)
                     state["w", e, which] = (wc, ws)
                 wc, ws = state["w", e, which]
-                on_v = (G * which + g) in (1, 4, 5)
+                on_v = (G * which + g) in ((1, 4, 5) if last else (1, 4, 5))
                 grp = grpv.tile([P, H, J], BF16, name="grp_v", align_bytes=64) if on_v else grpp.tile([P, H, J], BF16, name="grp_s", align_bytes=64)
                 src = raw[:].rearrange("p (j m t) -> p m t j", j=J, t=4)
                 dst = grp[:].rearrange("p (t m) j -> p m t j", t=4)
-                final = last and which == 1 and g == G - 1
                 m = (V_M_LAST if final else P) if on_v else 0
-                if m:
-                    nc.vector.tensor_copy(dst[:, :m], src[:, :m])
-                if m < P:
-                    nc.scalar.copy(dst[:, m:], src[:, m:])
+                for q in range(pieces):
+                    js = slice(q * J // pieces, (q + 1) * J // pieces)
+                    if m:
+                        nc.vector.tensor_copy(dst[:, :m, :, js], src[:, :m, :, js])
+                    if m < P:
+                        nc.scalar.copy(dst[:, m:, :, js], src[:, m:, :, js])
                 parts = 2 if final else 1
                 width = H // parts
                 jobs = [(wc[:, g, u * width:u * width + width], ws[:, g, u * width:u * width + width], grp[:, u * width:u * width + width, :]) for u in range(parts)]
-            for codes, scales, grouped in pending:
-                nc.vector.quantize_mx(out=codes.bitcast(FP8X4), scales=scales, in_=flat(grouped))
+            if not (last and which == 2):
+                for codes, scales, grouped in pending:
+                    nc.vector.quantize_mx(out=codes.bitcast(FP8X4), scales=scales, in_=flat(grouped))
             pending = jobs
             for due, function, args in later:
                 if due == step:

@@ -61,7 +61,7 @@ def tile_routed_moe_kernel(tc, xT, w1, w3, w2, gate, offs, out):
             nc.sync.dma_start(xraw[:], x_rows[g])
             if g == 0:
                 nc.sync.dma_start(lst[:], offs)
-            xin = xraw[:].rearrange("p (j n) -> p n j", j=J)
+            xin = xraw[:].rearrange("p (j c i) -> p c j i", j=J, i=4)
             xw = keep.tile([P, T], U32, name=f"xw{g}", align_bytes=64)
             xs = keep.tile([P, T], U8, name=f"xs{g}", align_bytes=64)
             for half in range(2):
@@ -69,10 +69,10 @@ def tile_routed_moe_kernel(tc, xT, w1, w3, w2, gate, offs, out):
                 cols = slice(t0, t0 + H)
                 if (g, half) in ((0, 0), (2, 0)):
                     grp = grpv.tile([P, H, J], BF16, name="grp_v", align_bytes=64)
-                    nc.vector.tensor_copy(grp[:], xin[:, cols, :])
+                    nc.vector.tensor_copy(grp[:].rearrange("p (c i) j -> p c j i", i=4), xin[:, t0 // 4:t0 // 4 + H // 4])
                 else:
                     grp = grpp.tile([P, H, J], BF16, name="grp_s", align_bytes=64)
-                    nc.scalar.copy(grp[:], xin[:, cols, :])
+                    nc.scalar.copy(grp[:].rearrange("p (c i) j -> p c j i", i=4), xin[:, t0 // 4:t0 // 4 + H // 4])
                 nc.vector.quantize_mx(out=xw[:, cols].bitcast(FP8X4), scales=xs[:, cols], in_=flat(grp[:]))
             nc.vector.tensor_copy(gw[:, g, :], xw[:].indirect(lst[:]))
             nc.vector.tensor_copy(gs[:, g, :], xs[:].indirect(lst[:]))
@@ -151,11 +151,12 @@ def tile_routed_moe_kernel(tc, xT, w1, w3, w2, gate, offs, out):
                 if e == 0:
                     nc.sync.dma_start(gt[:], gate.rearrange("(b p) s -> p b s", p=P))
                 grp = work.tile([P, N, J], BF16, name="grp2", align_bytes=64)
-                n0 = N // 2 if last else 0
-                src = raw[:].rearrange("p (j n) -> p n j", j=J)
+                n0 = N // 8 if last else 0
+                src = raw[:].rearrange("p (j c i) -> p c j i", j=J, i=4)
+                dst = grp[:].rearrange("p (c i) j -> p c j i", i=4)
                 if last:
-                    nc.vector.tensor_copy(grp[:, :n0], src[:, :n0])
-                nc.scalar.copy(grp[:, n0:], src[:, n0:])
+                    nc.vector.tensor_copy(dst[:, :n0], src[:, :n0])
+                nc.scalar.copy(dst[:, n0:], src[:, n0:])
                 vc = work.tile([P, N], U32, name="vc", align_bytes=64)
                 vs = work.tile([P, N], U8, name="vs", align_bytes=64)
                 state["w2", e] = (vc, vs)
@@ -172,17 +173,17 @@ def tile_routed_moe_kernel(tc, xT, w1, w3, w2, gate, offs, out):
                     ws = wq.tile([P, G, H], U8, name=f"ws{which}", align_bytes=64)
                     state["w", e, which] = (wc, ws)
                 wc, ws = state["w", e, which]
-                on_v = (G * which + g) in ((1, 4, 5) if last else (1, 4, 5))
+                on_v = (G * which + g) in ((1, 4, 5), (1, 4, 5), (1, 4, 5), (1, 4, 5))[e]
                 grp = grpv.tile([P, H, J], BF16, name="grp_v", align_bytes=64) if on_v else grpp.tile([P, H, J], BF16, name="grp_s", align_bytes=64)
-                src = raw[:].rearrange("p (j m t) -> p m t j", j=J, t=4)
-                dst = grp[:].rearrange("p (t m) j -> p m t j", t=4)
+                src = raw[:].rearrange("p (j m t) -> p m j t", j=J, t=4)
+                dst = grp[:].rearrange("p (t m) j -> p m j t", t=4)
                 m = (V_M_LAST if final else P) if on_v else 0
                 for q in range(pieces):
                     js = slice(q * J // pieces, (q + 1) * J // pieces)
                     if m:
-                        nc.vector.tensor_copy(dst[:, :m, :, js], src[:, :m, :, js])
+                        nc.vector.tensor_copy(dst[:, :m, js, :], src[:, :m, js, :])
                     if m < P:
-                        nc.scalar.copy(dst[:, m:, :, js], src[:, m:, :, js])
+                        nc.scalar.copy(dst[:, m:, js, :], src[:, m:, js, :])
                 parts = 2 if final else 1
                 width = H // parts
                 jobs = [(wc[:, g, u * width:u * width + width], ws[:, g, u * width:u * width + width], grp[:, u * width:u * width + width, :]) for u in range(parts)]

from contextlib import ExitStack

import concourse.mybir as mybir

K, T, E, C, H, N = 1536, 1024, 4, 128, 512, 256
S = E * C
P = 128
J = 4
G = K // (P * J)
NB = N // P

F32 = mybir.dt.float32
BF16 = mybir.dt.bfloat16
U32 = mybir.dt.uint32
U16 = mybir.dt.uint16
U8 = mybir.dt.uint8
FP8X4 = mybir.dt.float8_e4m3fn_x4
MULT = mybir.AluOpType.mult
SILU = mybir.ActivationFunctionType.Silu

V_M_LAST = 72

FLOPS = 2 * S * (2 * K * H + H * N)


def flat(grouped):
    return grouped.rearrange("p w j -> p (w j)")


def tile_routed_moe_kernel(tc, xT, w1, w3, w2, gate, offs, out):
    nc = tc.nc
    x_rows = xT.rearrange("(g p j) n -> g p (j n)", p=P, j=J)
    w_rows = [w.rearrange("e (g p j) h -> e g p (j h)", p=P, j=J) for w in (w1, w3)]
    w2_rows = w2.rearrange("e (p j) n -> e p (j n)", j=J)

    with ExitStack() as ctx:
        keep = ctx.enter_context(tc.tile_pool(name="keep", bufs=1))
        xrawp = ctx.enter_context(tc.tile_pool(name="xrawp", bufs=3))
        rawp = ctx.enter_context(tc.tile_pool(name="rawp", bufs=7))
        grpp = ctx.enter_context(tc.tile_pool(name="grpp", bufs=3))
        grpv = ctx.enter_context(tc.tile_pool(name="grpv", bufs=2))
        wq = ctx.enter_context(tc.tile_pool(name="wq", bufs=2))
        work = ctx.enter_context(tc.tile_pool(name="work", bufs=2))
        psum = ctx.enter_context(tc.psum_pool(name="psum", bufs=2))

        lst = keep.tile([P, S // 16], U16, name="lst")
        gt = keep.tile([P, NB, S], F32, name="gt")
        wins = []
        for b in range(NB):
            win = keep.tile([P, T], F32, name=f"win{b}")
            nc.vector.memset(win[:], 0.0)
            wins.append(win)
        warm = keep.tile([P, 1], F32, name="warm")
        nc.vector.memset(warm[:], 0.0)
        nc.scalar.activation(warm[:], warm[:], SILU)

        gw = keep.tile([P, G, S], U32, name="gw", align_bytes=64)
        gs = keep.tile([P, G, S], U8, name="gs", align_bytes=64)
        for g in range(G):
            xraw = xrawp.tile([P, J * T], F32, name="xraw")
            nc.sync.dma_start(xraw[:], x_rows[g])
            if g == 0:
                nc.sync.dma_start(lst[:], offs)
            xin = xraw[:].rearrange("p (j c i) -> p c j i", j=J, i=4)
            xw = keep.tile([P, T], U32, name=f"xw{g}", align_bytes=64)
            xs = keep.tile([P, T], U8, name=f"xs{g}", align_bytes=64)
            for half in range(2):
                t0 = half * H
                cols = slice(t0, t0 + H)
                if (g, half) in ((0, 0), (2, 0)):
                    grp = grpv.tile([P, H, J], BF16, name="grp_v", align_bytes=64)
                    nc.vector.tensor_copy(grp[:].rearrange("p (c i) j -> p c j i", i=4), xin[:, t0 // 4:t0 // 4 + H // 4])
                else:
                    grp = grpp.tile([P, H, J], BF16, name="grp_s", align_bytes=64)
                    nc.scalar.copy(grp[:].rearrange("p (c i) j -> p c j i", i=4), xin[:, t0 // 4:t0 // 4 + H // 4])
                nc.vector.quantize_mx(out=xw[:, cols].bitcast(FP8X4), scales=xs[:, cols], in_=flat(grp[:]))
            nc.vector.tensor_copy(gw[:, g, :], xw[:].indirect(lst[:]))
            nc.vector.tensor_copy(gs[:, g, :], xs[:].indirect(lst[:]))

        state = {}

        def slots(e):
            return slice(C * e, C * e + C)

        def first_layer(e, which):
            wc, ws = state["w", e, which]
            acc = psum.tile([P, 4, C], F32, name=f"acc{which}")
            for t in range(4):
                for g in range(G):
                    nc.tensor.matmul_mx(
                        out=acc[:, t, :],
                        lhsT=wc[:, g, P * t:P * t + P].bitcast(FP8X4),
                        lhsT_scale=ws[:, g, P * t:P * t + P],
                        rhs=gw[:, g, slots(e)].bitcast(FP8X4),
                        rhs_scale=gs[:, g, slots(e)],
                        start=(g == 0),
                        stop=(g == G - 1),
                    )
            state["acc", e, which] = acc

        def silu(e):
            sil = work.tile([P, 4, C], F32, name="sil")
            nc.scalar.activation(sil[:], state["acc", e, 0][:], SILU)
            state["sil", e] = sil

        def product(e):
            hb = work.tile([P, C, 4], BF16, name="hb", align_bytes=64)
            nc.vector.tensor_tensor(hb[:], state["sil", e][:].rearrange("p t c -> p c t"), state["acc", e, 1][:].rearrange("p t c -> p c t"), MULT)
            state["hb", e] = hb

        def quantise_hidden(e):
            hc = work.tile([P, C], U32, name="hc", align_bytes=64)
            hs = work.tile([P, C], U8, name="hs", align_bytes=64)
            nc.vector.quantize_mx(out=hc[:].bitcast(FP8X4), scales=hs[:], in_=flat(state["hb", e][:]))
            vc, vs = state["w2", e]
            y = psum.tile([P, NB, C], F32, name="y")
            for b in range(NB):
                nc.tensor.matmul_mx(
                    out=y[:, b, :],
                    lhsT=vc[:, P * b:P * b + P].bitcast(FP8X4),
                    lhsT_scale=vs[:, P * b:P * b + P],
                    rhs=hc[:].bitcast(FP8X4),
                    rhs_scale=hs[:],
                    start=True,
                    stop=True,
                )
            state["y", e] = y

        def gated(e):
            yg = work.tile([P, NB, C], F32, name="yg")
            nc.vector.tensor_tensor(yg[:], state["y", e][:], gt[:, :, slots(e)], MULT)
            state["yg", e] = yg

        def scatter(e, b):
            nc.vector.tensor_copy(wins[b][:].indirect(lst[:, 8 * e:8 * e + 8]), state["yg", e][:, b, :])

        items = []
        for e in range(E):
            items.extend([(e, which, g) for which in range(2) for g in range(G)])
            items.append((e, 2, 0))
        later = []
        pending = []
        for step, (e, which, g) in enumerate(items):
            last = e == E - 1
            if last and which == 2:
                for codes, scales, grouped in pending:
                    nc.vector.quantize_mx(out=codes.bitcast(FP8X4), scales=scales, in_=flat(grouped))
            if which == 2:
                raw = work.tile([P, J * N], F32, name="raw2")
                nc.sync.dma_start(raw[:], w2_rows[e])
                if e == 0:
                    nc.sync.dma_start(gt[:], gate.rearrange("(b p) s -> p b s", p=P))
                grp = work.tile([P, N, J], BF16, name="grp2", align_bytes=64)
                n0 = N // 8 if last else 0
                src = raw[:].rearrange("p (j c i) -> p c j i", j=J, i=4)
                dst = grp[:].rearrange("p (c i) j -> p c j i", i=4)
                if last:
                    nc.vector.tensor_copy(dst[:, :n0], src[:, :n0])
                nc.scalar.copy(dst[:, n0:], src[:, n0:])
                vc = work.tile([P, N], U32, name="vc", align_bytes=64)
                vs = work.tile([P, N], U8, name="vs", align_bytes=64)
                state["w2", e] = (vc, vs)
                jobs = [(vc[:], vs[:], grp[:])]
            else:
                final = last and which == 1 and g == G - 1
                raw = rawp.tile([P, J * H], F32, name="raw")
                pieces = 2 if final else 1
                for q in range(pieces):
                    part = slice(q * J * H // pieces, (q + 1) * J * H // pieces)
                    nc.sync.dma_start(raw[:, part], w_rows[which][e, g, :, part])
                if g == 0:
                    wc = wq.tile([P, G, H], U32, name=f"wc{which}", align_bytes=64)
                    ws = wq.tile([P, G, H], U8, name=f"ws{which}", align_bytes=64)
                    state["w", e, which] = (wc, ws)
                wc, ws = state["w", e, which]
                on_v = (G * which + g) in ((1, 4, 5), (1, 4, 5), (1, 4, 5), (1, 4, 5))[e]
                grp = grpv.tile([P, H, J], BF16, name="grp_v", align_bytes=64) if on_v else grpp.tile([P, H, J], BF16, name="grp_s", align_bytes=64)
                src = raw[:].rearrange("p (j m t) -> p m j t", j=J, t=4)
                dst = grp[:].rearrange("p (t m) j -> p m j t", t=4)
                m = (V_M_LAST if final else P) if on_v else 0
                for q in range(pieces):
                    js = slice(q * J // pieces, (q + 1) * J // pieces)
                    if m:
                        nc.vector.tensor_copy(dst[:, :m, js, :], src[:, :m, js, :])
                    if m < P:
                        nc.scalar.copy(dst[:, m:, js, :], src[:, m:, js, :])
                parts = 2 if final else 1
                width = H // parts
                jobs = [(wc[:, g, u * width:u * width + width], ws[:, g, u * width:u * width + width], grp[:, u * width:u * width + width, :]) for u in range(parts)]
            if not (last and which == 2):
                for codes, scales, grouped in pending:
                    nc.vector.quantize_mx(out=codes.bitcast(FP8X4), scales=scales, in_=flat(grouped))
            pending = jobs
            for due, function, args in later:
                if due == step:
                    function(*args)
            if which < 2 and g == G - 1:
                later.append((step + 1, first_layer, (e, which)))
                if which == 0:
                    later.append((step + 3, silu, (e,)))
                elif not last:
                    later.append((step + 2, product, (e,)))
                    later.append((step + 3, quantise_hidden, (e,)))
                    later.append((step + 4, gated, (e,)))
                    later.append((step + 5, scatter, (e, 0)))
                    later.append((step + 6, scatter, (e, 1)))
        for codes, scales, grouped in pending:
            nc.vector.quantize_mx(out=codes.bitcast(FP8X4), scales=scales, in_=flat(grouped))
        e = E - 1
        product(e)
        quantise_hidden(e)
        yg = work.tile([P, NB, C], F32, name="yg")
        for b in range(NB):
            nc.vector.tensor_tensor(yg[:, b, :], state["y", e][:, b, :], gt[:, b, slots(e)], MULT)
            state["yg", e] = yg
            scatter(e, b)
            nc.sync.dma_start(out[P * b:P * b + P, :], wins[b][:])
